import numpy as np
CORES = [0,1,2,3,4,5,6,7]
N = 8
def setup_inputs(rng):
    return {"x": rng.standard_normal((N, 128 // N, 8192), dtype=np.float32)}
def reference(x):
    g = np.concatenate(list(x), axis=0)
    return {"y": np.broadcast_to(g, (N,) + g.shape)}

from concourse.bass import DstId, RemoteDMATransfer

N = 8
P = 128 // N
ENGINES = 16

SCRATCH = {
    "land": ("dram", [N, 128, 1024], "float32"),
}
SEMAPHORES = ["loaded", "sent", "stored"] + ["arr%d" % j for j in range(N)]


def rank_program(g, core, T, topo):
    rank = T.rank_of(core)
    if rank is None:
        return
    cores = list(T.cores)

    g.sync.dma_start(T.land[rank], T.x[:, :]).then_inc(T.sem.loaded, 16)
    g.scalar.dma_start(T.y[P * rank:P * (rank + 1), :], T.x[:, :]).then_inc(T.sem.stored, 16)

    others = [(rank + d) % N for d in range(1, N)]
    ids = []
    for j in others:
        rid, pid, _se = topo.addr(cores[j])
        ids.append(DstId(rid=rid, pnc=pid))
    g.wait_ge(T.sem.loaded, 16)
    g.remote_dma_fused(
        [RemoteDMATransfer(
            dst_ids=ids,
            dma_engine_mask=topo.mask(core, cores[others[0]]),
            remote_sem=T.sem["arr%d" % rank],
            srcs=[T.land[rank]],
            dsts=[T.land[rank] for _j in others],
            alu_op=0,
        )],
        local_sem=T.sem.sent,
    )

    queues = [g.sync, g.scalar]
    for k, d in enumerate(range(1, N)):
        j = (rank - d) % N
        q = queues[k % 2]
        q.wait_ge(T.sem["arr%d" % j], ENGINES)
        q.dma_start(T.y[P * j:P * (j + 1), :], T.land[j]).then_inc(T.sem.stored, 16)

    g.wait_ge(T.sem.sent, ENGINES)
    g.wait_ge(T.sem.stored, 16 * N)
